import numpy as np, ml_dtypes
CORES = [17,57,65,89,97,121]
N = 6
F = 512
GROUPS = [[0,1,2],[3,4,5]]
def setup_inputs(rng):
    return {"x": rng.standard_normal((N, 128, F), dtype=np.float32).astype(ml_dtypes.bfloat16), "w": (rng.standard_normal((N, 128, 128), dtype=np.float32) / 11).astype(ml_dtypes.bfloat16)}
def setup_inputs_big(rng):
    d = setup_inputs(rng)
    for k in ("x", "w"): d[k] = (d[k].astype(np.float32) * 1024.0).astype(d[k].dtype)
    return d
def setup_inputs_small(rng):
    d = setup_inputs(rng)
    for k in ("x", "w"): d[k] = (d[k].astype(np.float32) * (1 / 1024.0)).astype(d[k].dtype)
    return d
def setup_inputs_apart(rng):
    d = setup_inputs(rng)
    f = (10.0 ** rng.permutation(np.linspace(-1.5, 1.5, N))).astype(np.float32).reshape(N, 1, 1)
    for k in ("x", "w"): d[k] = (d[k].astype(np.float32) * f).astype(d[k].dtype)
    return d
def reference(x, w):
    X, W = x.astype(np.float64), w.astype(np.float64)
    s = sum(W[g[0]].T @ np.maximum(sum(X[j] for j in g), 0.0) for g in GROUPS).astype(ml_dtypes.bfloat16)
    return {"y": np.broadcast_to(s, (N,) + s.shape)}

@@ -1,0 +1,233 @@
+from concourse.bass import DstId, RemoteDMATransfer
+from concourse.mybir import AluOpType
+
+NCORES = 128
+F, KW = 512, 128
+HM = (F + KW) // 2
+HC = F // 2
+HI = KW // 2
+
+SCRATCH = {
+    "XW": ("sbuf", [128, F + KW], "bfloat16"),
+    "LA": ("sbuf", [128, HM], "bfloat16"),
+    "LB": ("sbuf", [128, HM], "bfloat16"),
+    "M0": ("sbuf", [128, F + KW], "bfloat16"),
+    "M1": ("sbuf", [128, F + KW], "bfloat16"),
+    "C0": ("sbuf", [128, F], "bfloat16"),
+    "C1": ("sbuf", [128, F], "bfloat16"),
+    "ZI": ("sbuf", [128, KW + 1], "bfloat16"),
+    "DI": ("dram", [KW + 1, 128], "bfloat16"),
+    "ID": ("sbuf", [128, KW], "bfloat16"),
+    "ZERO": ("sbuf", [128, HC], "float32"),
+    "T0": ("sbuf", [128, F], "bfloat16"),
+    "T1": ("sbuf", [128, F], "bfloat16"),
+    "YS": ("sbuf", [128, F], "bfloat16"),
+    "PS00": ("psum", [128, 512], "float32"),
+    "PS01": ("psum", [128, 512], "float32"),
+    "PS10": ("psum", [128, 512], "float32"),
+    "PS11": ("psum", [128, 512], "float32"),
+    "PY0": ("psum", [128, 512], "float32"),
+    "PY1": ("psum", [128, 512], "float32"),
+}
+SEMAPHORES = ["ldx", "ldw", "zf", "fill", "id1", "id2", "sID", "hin", "sent", "sM0", "sM1", "sC0", "sC1",
+              "sum00", "sum01", "sum10", "sum11", "rel00", "rel01", "rel10", "rel11",
+              "sy0", "sy1", "cp0", "cp1", "st0", "st1"]
+
+
+def _bits(m):
+    return [e for e in range(16) if (m >> e) & 1]
+
+
+def _mask(engines):
+    m = 0
+    for e in engines:
+        m |= 1 << e
+    return m
+
+
+def _engines(topo, src, near, far):
+    off = _bits(topo.mask(src, far))
+    return off, [e for e in _bits(topo.mask(src, near)) if e not in off]
+
+
+def _tr(topo, dests, engines, sem, srcs, dst_ap, alu=0):
+    ids = [DstId(rid=topo.addr(d)[0], pnc=topo.addr(d)[1]) for d in dests]
+    return RemoteDMATransfer(dst_ids=ids, dma_engine_mask=_mask(engines), remote_sem=sem,
+                             srcs=srcs, dsts=[dst_ap for d in dests], alu_op=alu)
+
+
+def _helper(topo, cores, r, h):
+    for k in range(NCORES):
+        if (topo.chip(k) == topo.chip(r) and k not in cores and (topo.die(k) == topo.die(r)) == (h == 0)
+                and all(topo.may_write(k, d) for d in cores)):
+            return k
+    raise ValueError("no helper")
+
+
+def _plan(T, topo):
+    cores = list(T.cores)
+    info = []
+    for mem in T.tables["GROUPS"]:
+        a = cores[mem[0]]
+        rest = [cores[m] for m in mem[1:]]
+        near = [r for r in rest if topo.may_write(a, r)]
+        far = [r for r in rest if not topo.may_write(a, r)]
+        assert len(near) == 1 and len(far) == 1
+        info.append((a, near[0], far[0]))
+    return cores, info
+
+
+def _helper_program(g, core, T, topo, kind, gi, h, r, far, n_in):
+    S = T.sem
+    g.vector.memset(T.ZI[:, :], 0.0).then_inc(S.fill, 1)
+    g.vector.wait_ge(S.fill, 1)
+    g.vector.memset(T.ZI[:, 0:1], 1.0).then_inc(S.fill, 1)
+    g.sync.wait_ge(S.fill, 2)
+    g.sync.dma_start(T.DI[:, :], T.ZI[:, :]).then_inc(S.id1, 16)
+    g.sync.wait_ge(S.id1, 16)
+    g.sync.dma_start(T.ID[:, h * HI:(h + 1) * HI], T.DI[0:128, h * HI:(h + 1) * HI]).then_inc(S.id2, 16)
+    g.wait_ge(S.id2, 16)
+    m_on = topo.mask(core, r)
+    g.remote_dma(out_ap=T.ID[:, h * HI:(h + 1) * HI], in_ap=T.ID[:, h * HI:(h + 1) * HI], remote_sem=S.sID,
+                 local_sem=S.sent, pid=topo.addr(r)[1], routing_id=topo.addr(r)[0], dma_engine_mask=m_on)
+    sent = len(_bits(m_on))
+    off, only_on = _engines(topo, core, r, far[0])
+    g.wait_ge(S.hin, n_in)
+    if kind == "hub":
+        dst = T["M%d" % gi][:, h * HM:(h + 1) * HM]
+        srcs = [T.LA[:, :], T.LB[:, :]]
+        g.remote_dma_fused([_tr(topo, far, off, S["sM%d" % gi], srcs, dst, 1),
+                            _tr(topo, [r], only_on, S["sM%d" % gi], srcs, dst, 1)], local_sem=S.sent)
+        sent += len(off) + len(only_on)
+    else:
+        g.remote_dma_fused([_tr(topo, far, off, S["sC%d" % gi], [T.LA[:, 0:HC]],
+                                T["C%d" % gi][:, h * HC:(h + 1) * HC])], local_sem=S.sent)
+        sent += len(off)
+    g.wait_ge(S.sent, sent)
+
+
+def rank_program(g, core, T, topo):
+    cores, info = _plan(T, topo)
+    S = T.sem
+
+    def split(r, far):
+        off, on = _engines(topo, r, _helper(topo, cores, r, 0), far)
+        return off, on
+
+    if core not in cores:
+        for gi, (a, b, c) in enumerate(info):
+            a2, b2, c2 = info[1 - gi]
+            for h in (0, 1):
+                offa, ona = split(a, b)
+                offb, onb = split(b, a)
+                offc, onc = split(c, a2)
+                if core == _helper(topo, cores, a, h):
+                    _helper_program(g, core, T, topo, "hub", gi, h, a, [c2, c], len(ona) // 2 + len(offb) // 2)
+                if core == _helper(topo, cores, b, h):
+                    _helper_program(g, core, T, topo, "hub", gi, h, b, [a2, b2], len(onb) // 2 + len(offa) // 2)
+                if core == _helper(topo, cores, c, h):
+                    _helper_program(g, core, T, topo, "relay", gi, h, c, [a, b, c2], len((offc, onc)[h]))
+        return
+
+    gi = [i for i, t in enumerate(info) if core in t][0]
+    go = 1 - gi
+    a, b, c = info[gi]
+    a2, b2, c2 = info[go]
+    hlp = [_helper(topo, cores, core, h) for h in (0, 1)]
+    n_id = sum(len(_bits(topo.mask(k, core))) for k in hlp)
+
+    g.sync.dma_start(T.XW[:, 0:F], T.x[:, :]).then_inc(S.ldx, 16)
+    if core == a:
+        g.scalar.dma_start(T.XW[:, F:F + KW], T.w[:, :]).then_inc(S.ldw, 16)
+    if core == b:
+        g.vector.memset(T.XW[:, F:F + KW], 0.0).then_inc(S.zf, 1)
+    g.vector.memset(T.ZERO[:, :], 0.0).then_inc(S.fill, 1)
+
+    g.wait_ge(S.ldx, 16)
+    if core == c:
+        off, on = split(c, a2)
+        g.remote_dma_fused([_tr(topo, [hlp[h]], (off, on)[h], S.hin, [T.XW[:, h * HC:(h + 1) * HC]], T.LA[:, 0:HC])
+                            for h in (0, 1)], local_sem=S.sent)
+        g.remote_dma_fused([_tr(topo, [a2, b2], off, S["sC%d" % gi], [T.XW[:, 0:F]], T["C%d" % gi][:, :])],
+                           local_sem=S.sent)
+        sent = len(off) + len(on) + len(off)
+    else:
+        other = b if core == a else a
+        land = T.LA if core == a else T.LB
+        if core == a:
+            g.wait_ge(S.ldw, 16)
+        else:
+            g.wait_ge(S.zf, 1)
+        off, on = split(core, other)
+        no, nn = len(off) // 2, len(on) // 2
+        trs = []
+        for h in (0, 1):
+            src = [T.XW[:, h * HM:(h + 1) * HM]]
+            trs.append(_tr(topo, [_helper(topo, cores, other, h)], off[h * no:(h + 1) * no], S.hin, src, land[:, :]))
+            trs.append(_tr(topo, [hlp[h]], on[h * nn:(h + 1) * nn], S.hin, src, land[:, :]))
+        g.remote_dma_fused(trs, local_sem=S.sent)
+        sent = 2 * no + 2 * nn
+
+    def n_m(grp):
+        ga, gb = info[grp][0], info[grp][1]
+        tot = 0
+        for h in (0, 1):
+            if core in (ga, gb):
+                k = _helper(topo, cores, core, h)
+                tot += len(_engines(topo, k, core, info[1 - grp][0])[1])
+            else:
+                src_rank = ga if core in (info[1 - grp][2], info[grp][2]) else gb
+                k = _helper(topo, cores, src_rank, h)
+                tot += len(_bits(topo.mask(k, core)))
+        return tot
+
+    def n_c(grp):
+        gc = info[grp][2]
+        if topo.may_write(gc, core):
+            return len(_bits(topo.mask(gc, core)))
+        return sum(len(_bits(topo.mask(_helper(topo, cores, gc, h), core))) for h in (0, 1))
+
+    M = [T.M0, T.M1]
+    C = [T.C0, T.C1]
+    sM = [S.sM0, S.sM1]
+    sC = [S.sC0, S.sC1]
+    if core == c:
+        seq = [(gi, T.XW, S.ldx, 16, True), (go, C[go], sC[go], n_c(go), True),
+               (go, M[go], sM[go], n_m(go), False), (gi, M[gi], sM[gi], n_m(gi), False)]
+        fin = [go, gi]
+    else:
+        seq = [(go, C[go], sC[go], n_c(go), True), (gi, M[gi], sM[gi], n_m(gi), True),
+               (gi, C[gi], sC[gi], n_c(gi), False), (go, M[go], sM[go], n_m(go), False)]
+        fin = [gi, go]
+
+    te, ve = g.tensor, g.vector
+    TT = [T.T0, T.T1]
+    PY = [T.PY0, T.PY1]
+    te.wait_ge(S.sID, n_id)
+    for grp, piece, sem, cnt, first in seq:
+        te.wait_ge(sem, cnt)
+        for ch in (0, 1):
+            mm = te.matmul(T["PS%d%d" % (grp, ch)][:, 0:HC], T.ID[:, :], piece[:, ch * HC:(ch + 1) * HC],
+                           first, not first)
+            if not first:
+                mm.then_inc(S["sum%d%d" % (grp, ch)], 1)
+    for i, grp in enumerate(fin):
+        for ch in (0, 1):
+            te.wait_ge(S["rel%d%d" % (grp, ch)], 1)
+            mm = te.matmul(PY[ch][:, 0:HC], M[grp][:, F:F + KW], TT[grp][:, ch * HC:(ch + 1) * HC], i == 0, i == 1)
+            if i == 1:
+                mm.then_inc(S["sy%d" % ch], 1)
+    ve.wait_ge(S.fill, 1)
+    for grp in fin:
+        for ch in (0, 1):
+            ve.wait_ge(S["sum%d%d" % (grp, ch)], 1)
+            ve.tensor_tensor(TT[grp][:, ch * HC:(ch + 1) * HC], T["PS%d%d" % (grp, ch)][:, 0:HC], T.ZERO[:, :],
+                             AluOpType.max).then_inc(S["rel%d%d" % (grp, ch)], 1)
+    for ch in (0, 1):
+        ve.wait_ge(S["sy%d" % ch], 1)
+        ve.tensor_copy(T.YS[:, ch * HC:(ch + 1) * HC], PY[ch][:, 0:HC]).then_inc(S["cp%d" % ch], 1)
+    for ch, q in ((0, g.sync), (1, g.scalar)):
+        q.wait_ge(S["cp%d" % ch], 1)
+        q.dma_start(T.y[:, ch * HC:(ch + 1) * HC], T.YS[:, ch * HC:(ch + 1) * HC]).then_inc(S["st%d" % ch], 16)
+        q.wait_ge(S["st%d" % ch], 16)
+    g.wait_ge(S.sent, sent)

@@ -3,34 +3,34 @@ from concourse.mybir import AluOpType
 
 NCORES = 128
 F, KW = 512, 128
-HM = (F + KW) // 2
 HC = F // 2
-HI = KW // 2
 
 SCRATCH = {
-    "XW": ("sbuf", [128, F + KW], "bfloat16"),
-    "LA": ("sbuf", [128, HM], "bfloat16"),
-    "LB": ("sbuf", [128, HM], "bfloat16"),
-    "M0": ("sbuf", [128, F + KW], "bfloat16"),
-    "M1": ("sbuf", [128, F + KW], "bfloat16"),
+    "X": ("sbuf", [128, F], "bfloat16"),
+    "LA": ("sbuf", [128, HC], "bfloat16"),
+    "LB": ("sbuf", [128, HC], "bfloat16"),
+    "WL": ("sbuf", [128, KW], "bfloat16"),
+    "M0": ("sbuf", [128, F], "bfloat16"),
+    "M1": ("sbuf", [128, F], "bfloat16"),
     "C0": ("sbuf", [128, F], "bfloat16"),
     "C1": ("sbuf", [128, F], "bfloat16"),
+    "WB0": ("sbuf", [128, KW], "bfloat16"),
+    "WB1": ("sbuf", [128, KW], "bfloat16"),
     "ZI": ("sbuf", [128, KW + 1], "bfloat16"),
     "DI": ("dram", [KW + 1, 128], "bfloat16"),
     "ID": ("sbuf", [128, KW], "bfloat16"),
-    "ZERO": ("sbuf", [128, HC], "float32"),
-    "T0": ("sbuf", [128, F], "bfloat16"),
-    "T1": ("sbuf", [128, F], "bfloat16"),
+    "U0": ("sbuf", [128, F], "bfloat16"),
+    "U1": ("sbuf", [128, F], "bfloat16"),
     "YS": ("sbuf", [128, F], "bfloat16"),
-    "PS00": ("psum", [128, 512], "float32"),
-    "PS01": ("psum", [128, 512], "float32"),
-    "PS10": ("psum", [128, 512], "float32"),
-    "PS11": ("psum", [128, 512], "float32"),
+    "NE00": ("psum", [128, 512], "float32"),
+    "NE01": ("psum", [128, 512], "float32"),
+    "NE10": ("psum", [128, 512], "float32"),
+    "NE11": ("psum", [128, 512], "float32"),
     "PY0": ("psum", [128, 512], "float32"),
     "PY1": ("psum", [128, 512], "float32"),
 }
-SEMAPHORES = ["ldx", "ldw", "zf", "fill", "id1", "id2", "sID", "hin", "sent", "sM0", "sM1", "sC0", "sC1",
-              "sum00", "sum01", "sum10", "sum11", "rel00", "rel01", "rel10", "rel11",
+SEMAPHORES = ["ldx", "ldw", "fill", "id1", "id2", "sID", "hin", "sent", "sM0", "sM1", "sC0", "sC1", "sW0", "sW1",
+              "ne00", "ne01", "ne10", "ne11", "u00", "u01", "u10", "u11",
               "sy0", "sy1", "cp0", "cp1", "st0", "st1"]
 
 
@@ -77,31 +77,55 @@ def _plan(T, topo):
     return cores, info
 
 
-def _helper_program(g, core, T, topo, kind, gi, h, r, far, n_in):
+def _wplan(topo, cores, info, gi):
+    a = info[gi][0]
+    cross = [d for d in cores if d != a and not topo.may_write(a, d)]
+    plane = [d for d in cores if d != a and topo.may_write(a, d)]
+    used = [_helper(topo, cores, a, h) for h in (0, 1)]
+    cand = [k for k in range(NCORES) if topo.chip(k) == topo.chip(a) and k not in cores and k not in used]
+    cand = [k for k in cand if topo.die(k) != topo.die(a)] + [k for k in cand if topo.die(k) == topo.die(a)]
+    p = [k for k in cand if all(topo.may_write(k, d) for d in cross)][0]
+    q = [k for k in cand if k != p and all(topo.may_write(k, d) for d in plane)][0]
+    return (p, cross), (q, plane)
+
+
+def _chip_helpers(topo, cores, info, r):
+    hl = [_helper(topo, cores, r, h) for h in (0, 1)]
+    for gi, t in enumerate(info):
+        if r == t[0]:
+            hl += [k for k, d in _wplan(topo, cores, info, gi)]
+    return hl
+
+
+def _helper_program(g, core, T, topo, kind, gi, h, r, far, n_in, lo, hi):
     S = T.sem
     g.vector.memset(T.ZI[:, :], 0.0).then_inc(S.fill, 1)
     g.vector.wait_ge(S.fill, 1)
-    g.vector.memset(T.ZI[:, 0:1], 1.0).then_inc(S.fill, 1)
+    g.vector.memset(T.ZI[:, 0:1], -1.0).then_inc(S.fill, 1)
     g.sync.wait_ge(S.fill, 2)
     g.sync.dma_start(T.DI[:, :], T.ZI[:, :]).then_inc(S.id1, 16)
     g.sync.wait_ge(S.id1, 16)
-    g.sync.dma_start(T.ID[:, h * HI:(h + 1) * HI], T.DI[0:128, h * HI:(h + 1) * HI]).then_inc(S.id2, 16)
+    g.sync.dma_start(T.ID[:, lo:hi], T.DI[0:128, lo:hi]).then_inc(S.id2, 16)
     g.wait_ge(S.id2, 16)
     m_on = topo.mask(core, r)
-    g.remote_dma(out_ap=T.ID[:, h * HI:(h + 1) * HI], in_ap=T.ID[:, h * HI:(h + 1) * HI], remote_sem=S.sID,
+    g.remote_dma(out_ap=T.ID[:, lo:hi], in_ap=T.ID[:, lo:hi], remote_sem=S.sID,
                  local_sem=S.sent, pid=topo.addr(r)[1], routing_id=topo.addr(r)[0], dma_engine_mask=m_on)
     sent = len(_bits(m_on))
     off, only_on = _engines(topo, core, r, far[0])
     g.wait_ge(S.hin, n_in)
     if kind == "hub":
-        dst = T["M%d" % gi][:, h * HM:(h + 1) * HM]
+        dst = T["M%d" % gi][:, h * HC:(h + 1) * HC]
         srcs = [T.LA[:, :], T.LB[:, :]]
         g.remote_dma_fused([_tr(topo, far, off, S["sM%d" % gi], srcs, dst, 1),
                             _tr(topo, [r], only_on, S["sM%d" % gi], srcs, dst, 1)], local_sem=S.sent)
         sent += len(off) + len(only_on)
-    else:
-        g.remote_dma_fused([_tr(topo, far, off, S["sC%d" % gi], [T.LA[:, 0:HC]],
+    elif kind == "relay":
+        g.remote_dma_fused([_tr(topo, far, off, S["sC%d" % gi], [T.LA[:, :]],
                                 T["C%d" % gi][:, h * HC:(h + 1) * HC])], local_sem=S.sent)
+        sent += len(off)
+    else:
+        g.remote_dma_fused([_tr(topo, far, off, S["sW%d" % gi], [T.WL[:, :]], T["WB%d" % gi][:, :])],
+                           local_sem=S.sent)
         sent += len(off)
     g.wait_ge(S.sent, sent)
 
@@ -111,22 +135,33 @@ def rank_program(g, core, T, topo):
     S = T.sem
 
     def split(r, far):
-        off, on = _engines(topo, r, _helper(topo, cores, r, 0), far)
-        return off, on
+        return _engines(topo, r, _helper(topo, cores, r, 0), far)
+
+    def share(r, k):
+        hl = _chip_helpers(topo, cores, info, r)
+        wd = KW // len(hl)
+        return hl.index(k) * wd, (hl.index(k) + 1) * wd
 
     if core not in cores:
         for gi, (a, b, c) in enumerate(info):
             a2, b2, c2 = info[1 - gi]
+            offa, ona = split(a, b)
+            offb, onb = split(b, a)
+            offc, onc = split(c, a2)
             for h in (0, 1):
-                offa, ona = split(a, b)
-                offb, onb = split(b, a)
-                offc, onc = split(c, a2)
                 if core == _helper(topo, cores, a, h):
-                    _helper_program(g, core, T, topo, "hub", gi, h, a, [c2, c], len(ona) // 2 + len(offb) // 2)
+                    lo, hi = share(a, core)
+                    _helper_program(g, core, T, topo, "hub", gi, h, a, [c2, c], len(ona) // 2 + len(offb) // 2, lo, hi)
                 if core == _helper(topo, cores, b, h):
-                    _helper_program(g, core, T, topo, "hub", gi, h, b, [a2, b2], len(onb) // 2 + len(offa) // 2)
+                    lo, hi = share(b, core)
+                    _helper_program(g, core, T, topo, "hub", gi, h, b, [a2, b2], len(onb) // 2 + len(offa) // 2, lo, hi)
                 if core == _helper(topo, cores, c, h):
-                    _helper_program(g, core, T, topo, "relay", gi, h, c, [a, b, c2], len((offc, onc)[h]))
+                    lo, hi = share(c, core)
+                    _helper_program(g, core, T, topo, "relay", gi, h, c, [a, b, c2], len((offc, onc)[h]), lo, hi)
+            for i, (k, dests) in enumerate(_wplan(topo, cores, info, gi)):
+                if core == k:
+                    lo, hi = share(a, core)
+                    _helper_program(g, core, T, topo, "w", gi, 0, a, dests, len((offa, ona)[i]), lo, hi)
         return
 
     gi = [i for i, t in enumerate(info) if core in t][0]
@@ -134,39 +169,44 @@ def rank_program(g, core, T, topo):
     a, b, c = info[gi]
     a2, b2, c2 = info[go]
     hlp = [_helper(topo, cores, core, h) for h in (0, 1)]
-    n_id = sum(len(_bits(topo.mask(k, core))) for k in hlp)
+    n_id = sum(len(_bits(topo.mask(k, core))) for k in _chip_helpers(topo, cores, info, core))
+    M = [T.M0, T.M1]
+    C = [T.C0, T.C1]
+    W = [T.WB0, T.WB1]
+    sM = [S.sM0, S.sM1]
+    sC = [S.sC0, S.sC1]
+    sW = [S.sW0, S.sW1]
 
-    g.sync.dma_start(T.XW[:, 0:F], T.x[:, :]).then_inc(S.ldx, 16)
+    g.sync.dma_start(T.X[:, :], T.x[:, :]).then_inc(S.ldx, 16)
     if core == a:
-        g.scalar.dma_start(T.XW[:, F:F + KW], T.w[:, :]).then_inc(S.ldw, 16)
-    if core == b:
-        g.vector.memset(T.XW[:, F:F + KW], 0.0).then_inc(S.zf, 1)
-    g.vector.memset(T.ZERO[:, :], 0.0).then_inc(S.fill, 1)
+        g.scalar.dma_start(W[gi][:, :], T.w[:, :]).then_inc(S.ldw, 16)
 
+    sent = 0
+    if core == a:
+        off, on = split(a, b)
+        g.wait_ge(S.ldw, 16)
+        g.remote_dma_fused([_tr(topo, [k], (off, on)[i], S.hin, [W[gi][:, :]], T.WL[:, :])
+                            for i, (k, dests) in enumerate(_wplan(topo, cores, info, gi))], local_sem=S.sent)
+        sent += len(off) + len(on)
     g.wait_ge(S.ldx, 16)
     if core == c:
         off, on = split(c, a2)
-        g.remote_dma_fused([_tr(topo, [hlp[h]], (off, on)[h], S.hin, [T.XW[:, h * HC:(h + 1) * HC]], T.LA[:, 0:HC])
+        g.remote_dma_fused([_tr(topo, [hlp[h]], (off, on)[h], S.hin, [T.X[:, h * HC:(h + 1) * HC]], T.LA[:, :])
                             for h in (0, 1)], local_sem=S.sent)
-        g.remote_dma_fused([_tr(topo, [a2, b2], off, S["sC%d" % gi], [T.XW[:, 0:F]], T["C%d" % gi][:, :])],
-                           local_sem=S.sent)
-        sent = len(off) + len(on) + len(off)
+        g.remote_dma_fused([_tr(topo, [a2, b2], off, sC[gi], [T.X[:, :]], C[gi][:, :])], local_sem=S.sent)
+        sent += len(off) + len(on) + len(off)
     else:
         other = b if core == a else a
         land = T.LA if core == a else T.LB
-        if core == a:
-            g.wait_ge(S.ldw, 16)
-        else:
-            g.wait_ge(S.zf, 1)
         off, on = split(core, other)
         no, nn = len(off) // 2, len(on) // 2
         trs = []
         for h in (0, 1):
-            src = [T.XW[:, h * HM:(h + 1) * HM]]
+            src = [T.X[:, h * HC:(h + 1) * HC]]
             trs.append(_tr(topo, [_helper(topo, cores, other, h)], off[h * no:(h + 1) * no], S.hin, src, land[:, :]))
             trs.append(_tr(topo, [hlp[h]], on[h * nn:(h + 1) * nn], S.hin, src, land[:, :]))
         g.remote_dma_fused(trs, local_sem=S.sent)
-        sent = 2 * no + 2 * nn
+        sent += 2 * no + 2 * nn
 
     def n_m(grp):
         ga, gb = info[grp][0], info[grp][1]
@@ -187,42 +227,49 @@ def rank_program(g, core, T, topo):
             return len(_bits(topo.mask(gc, core)))
         return sum(len(_bits(topo.mask(_helper(topo, cores, gc, h), core))) for h in (0, 1))
 
-    M = [T.M0, T.M1]
-    C = [T.C0, T.C1]
-    sM = [S.sM0, S.sM1]
-    sC = [S.sC0, S.sC1]
+    def w_wait(grp):
+        if core == info[grp][0]:
+            return S.ldw, 16
+        for k, dests in _wplan(topo, cores, info, grp):
+            if core in dests:
+                return sW[grp], len(_bits(topo.mask(k, core)))
+        raise ValueError("no W")
+
+    E, L = {}, {}
     if core == c:
-        seq = [(gi, T.XW, S.ldx, 16, True), (go, C[go], sC[go], n_c(go), True),
-               (go, M[go], sM[go], n_m(go), False), (gi, M[gi], sM[gi], n_m(gi), False)]
-        fin = [go, gi]
+        E[gi], L[gi] = (T.X, S.ldx, 16), (M[gi], sM[gi], n_m(gi))
     else:
-        seq = [(go, C[go], sC[go], n_c(go), True), (gi, M[gi], sM[gi], n_m(gi), True),
-               (gi, C[gi], sC[gi], n_c(gi), False), (go, M[go], sM[go], n_m(go), False)]
-        fin = [gi, go]
+        E[gi], L[gi] = (M[gi], sM[gi], n_m(gi)), (C[gi], sC[gi], n_c(gi))
+    E[go], L[go] = (C[go], sC[go], n_c(go)), (M[go], sM[go], n_m(go))
+    order = [gi, go]
 
     te, ve = g.tensor, g.vector
-    TT = [T.T0, T.T1]
+    U = [T.U0, T.U1]
     PY = [T.PY0, T.PY1]
     te.wait_ge(S.sID, n_id)
-    for grp, piece, sem, cnt, first in seq:
+    for i, grp in enumerate(order):
+        piece, sem, cnt = E[grp]
         te.wait_ge(sem, cnt)
         for ch in (0, 1):
-            mm = te.matmul(T["PS%d%d" % (grp, ch)][:, 0:HC], T.ID[:, :], piece[:, ch * HC:(ch + 1) * HC],
-                           first, not first)
-            if not first:
-                mm.then_inc(S["sum%d%d" % (grp, ch)], 1)
-    for i, grp in enumerate(fin):
+            te.matmul(T["NE%d%d" % (grp, ch)][:, 0:HC], T.ID[:, :], piece[:, ch * HC:(ch + 1) * HC],
+                      True, True).then_inc(S["ne%d%d" % (grp, ch)], 1)
+        ws, wc = w_wait(grp)
+        te.wait_ge(ws, wc)
         for ch in (0, 1):
-            te.wait_ge(S["rel%d%d" % (grp, ch)], 1)
-            mm = te.matmul(PY[ch][:, 0:HC], M[grp][:, F:F + KW], TT[grp][:, ch * HC:(ch + 1) * HC], i == 0, i == 1)
+            te.matmul(PY[ch][:, 0:HC], W[grp][:, :], piece[:, ch * HC:(ch + 1) * HC], i == 0, False)
+    for i, grp in enumerate(order):
+        for ch in (0, 1):
+            te.wait_ge(S["u%d%d" % (grp, ch)], 1)
+            mm = te.matmul(PY[ch][:, 0:HC], W[grp][:, :], U[grp][:, ch * HC:(ch + 1) * HC], False, i == 1)
             if i == 1:
                 mm.then_inc(S["sy%d" % ch], 1)
-    ve.wait_ge(S.fill, 1)
-    for grp in fin:
+    for grp in order:
+        piece, sem, cnt = L[grp]
+        ve.wait_ge(sem, cnt)
         for ch in (0, 1):
-            ve.wait_ge(S["sum%d%d" % (grp, ch)], 1)
-            ve.tensor_tensor(TT[grp][:, ch * HC:(ch + 1) * HC], T["PS%d%d" % (grp, ch)][:, 0:HC], T.ZERO[:, :],
-                             AluOpType.max).then_inc(S["rel%d%d" % (grp, ch)], 1)
+            ve.wait_ge(S["ne%d%d" % (grp, ch)], 1)
+            ve.tensor_tensor(U[grp][:, ch * HC:(ch + 1) * HC], T["NE%d%d" % (grp, ch)][:, 0:HC],
+                             piece[:, ch * HC:(ch + 1) * HC], AluOpType.max).then_inc(S["u%d%d" % (grp, ch)], 1)
     for ch in (0, 1):
         ve.wait_ge(S["sy%d" % ch], 1)
         ve.tensor_copy(T.YS[:, ch * HC:(ch + 1) * HC], PY[ch][:, 0:HC]).then_inc(S["cp%d" % ch], 1)

from concourse.bass import DstId, RemoteDMATransfer
from concourse.mybir import AluOpType

NCORES = 128
F, KW = 512, 128
HC = F // 2

SCRATCH = {
    "X": ("sbuf", [128, F], "bfloat16"),
    "LA": ("sbuf", [128, HC], "bfloat16"),
    "LB": ("sbuf", [128, HC], "bfloat16"),
    "WL": ("sbuf", [128, KW], "bfloat16"),
    "M0": ("sbuf", [128, F], "bfloat16"),
    "M1": ("sbuf", [128, F], "bfloat16"),
    "C0": ("sbuf", [128, F], "bfloat16"),
    "C1": ("sbuf", [128, F], "bfloat16"),
    "WB0": ("sbuf", [128, KW], "bfloat16"),
    "WB1": ("sbuf", [128, KW], "bfloat16"),
    "ZI": ("sbuf", [128, KW + 1], "bfloat16"),
    "DI": ("dram", [KW + 1, 128], "bfloat16"),
    "ID": ("sbuf", [128, KW], "bfloat16"),
    "U0": ("sbuf", [128, F], "bfloat16"),
    "U1": ("sbuf", [128, F], "bfloat16"),
    "YS": ("sbuf", [128, F], "bfloat16"),
    "NE00": ("psum", [128, 512], "float32"),
    "NE01": ("psum", [128, 512], "float32"),
    "NE10": ("psum", [128, 512], "float32"),
    "NE11": ("psum", [128, 512], "float32"),
    "PY0": ("psum", [128, 512], "float32"),
    "PY1": ("psum", [128, 512], "float32"),
}
SEMAPHORES = ["ldx", "ldw", "fill", "id1", "id2", "sID", "hin", "sent", "sM0", "sM1", "sC0", "sC1", "sW0", "sW1",
              "ne00", "ne01", "ne10", "ne11", "u00", "u01", "u10", "u11",
              "sy0", "sy1", "cp0", "cp1", "st0", "st1"]


def _bits(m):
    return [e for e in range(16) if (m >> e) & 1]


def _mask(engines):
    m = 0
    for e in engines:
        m |= 1 << e
    return m


def _engines(topo, src, near, far):
    off = _bits(topo.mask(src, far))
    return off, [e for e in _bits(topo.mask(src, near)) if e not in off]


def _tr(topo, dests, engines, sem, srcs, dst_ap, alu=0):
    ids = [DstId(rid=topo.addr(d)[0], pnc=topo.addr(d)[1]) for d in dests]
    return RemoteDMATransfer(dst_ids=ids, dma_engine_mask=_mask(engines), remote_sem=sem,
                             srcs=srcs, dsts=[dst_ap for d in dests], alu_op=alu)


def _helper(topo, cores, r, h):
    for k in range(NCORES):
        if (topo.chip(k) == topo.chip(r) and k not in cores and (topo.die(k) == topo.die(r)) == (h == 0)
                and all(topo.may_write(k, d) for d in cores)):
            return k
    raise ValueError("no helper")


def _plan(T, topo):
    cores = list(T.cores)
    info = []
    for mem in T.tables["GROUPS"]:
        a = cores[mem[0]]
        rest = [cores[m] for m in mem[1:]]
        near = [r for r in rest if topo.may_write(a, r)]
        far = [r for r in rest if not topo.may_write(a, r)]
        assert len(near) == 1 and len(far) == 1
        info.append((a, near[0], far[0]))
    return cores, info


def _wplan(topo, cores, info, gi):
    a = info[gi][0]
    cross = [d for d in cores if d != a and not topo.may_write(a, d)]
    plane = [d for d in cores if d != a and topo.may_write(a, d)]
    used = [_helper(topo, cores, a, h) for h in (0, 1)]
    cand = [k for k in range(NCORES) if topo.chip(k) == topo.chip(a) and k not in cores and k not in used]
    cand = [k for k in cand if topo.die(k) != topo.die(a)] + [k for k in cand if topo.die(k) == topo.die(a)]
    p = [k for k in cand if all(topo.may_write(k, d) for d in cross)][0]
    q = [k for k in cand if k != p and all(topo.may_write(k, d) for d in plane)][0]
    return (p, cross), (q, plane)


def _chip_helpers(topo, cores, info, r):
    hl = [_helper(topo, cores, r, h) for h in (0, 1)]
    for gi, t in enumerate(info):
        if r == t[0]:
            hl += [k for k, d in _wplan(topo, cores, info, gi)]
    return hl


def _helper_program(g, core, T, topo, kind, gi, h, r, far, n_in, lo, hi):
    S = T.sem
    g.vector.memset(T.ZI[:, :], 0.0).then_inc(S.fill, 1)
    g.vector.wait_ge(S.fill, 1)
    g.vector.memset(T.ZI[:, 0:1], -1.0).then_inc(S.fill, 1)
    g.sync.wait_ge(S.fill, 2)
    g.sync.dma_start(T.DI[:, :], T.ZI[:, :]).then_inc(S.id1, 16)
    g.sync.wait_ge(S.id1, 16)
    g.sync.dma_start(T.ID[:, lo:hi], T.DI[0:128, lo:hi]).then_inc(S.id2, 16)
    g.wait_ge(S.id2, 16)
    m_on = topo.mask(core, r)
    g.remote_dma(out_ap=T.ID[:, lo:hi], in_ap=T.ID[:, lo:hi], remote_sem=S.sID,
                 local_sem=S.sent, pid=topo.addr(r)[1], routing_id=topo.addr(r)[0], dma_engine_mask=m_on)
    sent = len(_bits(m_on))
    off, only_on = _engines(topo, core, r, far[0])
    g.wait_ge(S.hin, n_in)
    if kind == "hub":
        dst = T["M%d" % gi][:, h * HC:(h + 1) * HC]
        srcs = [T.LA[:, :], T.LB[:, :]]
        g.remote_dma_fused([_tr(topo, far, off, S["sM%d" % gi], srcs, dst, 1),
                            _tr(topo, [r], only_on, S["sM%d" % gi], srcs, dst, 1)], local_sem=S.sent)
        sent += len(off) + len(only_on)
    elif kind == "relay":
        g.remote_dma_fused([_tr(topo, far, off, S["sC%d" % gi], [T.LA[:, :]],
                                T["C%d" % gi][:, h * HC:(h + 1) * HC])], local_sem=S.sent)
        sent += len(off)
    else:
        g.remote_dma_fused([_tr(topo, far, off, S["sW%d" % gi], [T.WL[:, :]], T["WB%d" % gi][:, :])],
                           local_sem=S.sent)
        sent += len(off)
    g.wait_ge(S.sent, sent)


def rank_program(g, core, T, topo):
    cores, info = _plan(T, topo)
    S = T.sem

    def split(r, far):
        return _engines(topo, r, _helper(topo, cores, r, 0), far)

    def share(r, k):
        hl = _chip_helpers(topo, cores, info, r)
        wd = KW // len(hl)
        return hl.index(k) * wd, (hl.index(k) + 1) * wd

    if core not in cores:
        for gi, (a, b, c) in enumerate(info):
            a2, b2, c2 = info[1 - gi]
            offa, ona = split(a, b)
            offb, onb = split(b, a)
            offc, onc = split(c, a2)
            for h in (0, 1):
                if core == _helper(topo, cores, a, h):
                    lo, hi = share(a, core)
                    _helper_program(g, core, T, topo, "hub", gi, h, a, [c2, c], len(ona) // 2 + len(offb) // 2, lo, hi)
                if core == _helper(topo, cores, b, h):
                    lo, hi = share(b, core)
                    _helper_program(g, core, T, topo, "hub", gi, h, b, [a2, b2], len(onb) // 2 + len(offa) // 2, lo, hi)
                if core == _helper(topo, cores, c, h):
                    lo, hi = share(c, core)
                    _helper_program(g, core, T, topo, "relay", gi, h, c, [a, b, c2], len((offc, onc)[h]), lo, hi)
            for i, (k, dests) in enumerate(_wplan(topo, cores, info, gi)):
                if core == k:
                    lo, hi = share(a, core)
                    _helper_program(g, core, T, topo, "w", gi, 0, a, dests, len((offa, ona)[i]), lo, hi)
        return

    gi = [i for i, t in enumerate(info) if core in t][0]
    go = 1 - gi
    a, b, c = info[gi]
    a2, b2, c2 = info[go]
    hlp = [_helper(topo, cores, core, h) for h in (0, 1)]
    n_id = sum(len(_bits(topo.mask(k, core))) for k in _chip_helpers(topo, cores, info, core))
    M = [T.M0, T.M1]
    C = [T.C0, T.C1]
    W = [T.WB0, T.WB1]
    sM = [S.sM0, S.sM1]
    sC = [S.sC0, S.sC1]
    sW = [S.sW0, S.sW1]

    g.sync.dma_start(T.X[:, :], T.x[:, :]).then_inc(S.ldx, 16)
    if core == a:
        g.scalar.dma_start(W[gi][:, :], T.w[:, :]).then_inc(S.ldw, 16)

    sent = 0
    if core == a:
        off, on = split(a, b)
        g.wait_ge(S.ldw, 16)
        g.remote_dma_fused([_tr(topo, [k], (off, on)[i], S.hin, [W[gi][:, :]], T.WL[:, :])
                            for i, (k, dests) in enumerate(_wplan(topo, cores, info, gi))], local_sem=S.sent)
        sent += len(off) + len(on)
    g.wait_ge(S.ldx, 16)
    if core == c:
        off, on = split(c, a2)
        g.remote_dma_fused([_tr(topo, [hlp[h]], (off, on)[h], S.hin, [T.X[:, h * HC:(h + 1) * HC]], T.LA[:, :])
                            for h in (0, 1)], local_sem=S.sent)
        g.remote_dma_fused([_tr(topo, [a2, b2], off, sC[gi], [T.X[:, :]], C[gi][:, :])], local_sem=S.sent)
        sent += len(off) + len(on) + len(off)
    else:
        other = b if core == a else a
        land = T.LA if core == a else T.LB
        off, on = split(core, other)
        no, nn = len(off) // 2, len(on) // 2
        trs = []
        for h in (0, 1):
            src = [T.X[:, h * HC:(h + 1) * HC]]
            trs.append(_tr(topo, [_helper(topo, cores, other, h)], off[h * no:(h + 1) * no], S.hin, src, land[:, :]))
            trs.append(_tr(topo, [hlp[h]], on[h * nn:(h + 1) * nn], S.hin, src, land[:, :]))
        g.remote_dma_fused(trs, local_sem=S.sent)
        sent += 2 * no + 2 * nn

    def n_m(grp):
        ga, gb = info[grp][0], info[grp][1]
        tot = 0
        for h in (0, 1):
            if core in (ga, gb):
                k = _helper(topo, cores, core, h)
                tot += len(_engines(topo, k, core, info[1 - grp][0])[1])
            else:
                src_rank = ga if core in (info[1 - grp][2], info[grp][2]) else gb
                k = _helper(topo, cores, src_rank, h)
                tot += len(_bits(topo.mask(k, core)))
        return tot

    def n_c(grp):
        gc = info[grp][2]
        if topo.may_write(gc, core):
            return len(_bits(topo.mask(gc, core)))
        return sum(len(_bits(topo.mask(_helper(topo, cores, gc, h), core))) for h in (0, 1))

    def w_wait(grp):
        if core == info[grp][0]:
            return S.ldw, 16
        for k, dests in _wplan(topo, cores, info, grp):
            if core in dests:
                return sW[grp], len(_bits(topo.mask(k, core)))
        raise ValueError("no W")

    E, L = {}, {}
    if core == c:
        E[gi], L[gi] = (T.X, S.ldx, 16), (M[gi], sM[gi], n_m(gi))
    else:
        E[gi], L[gi] = (M[gi], sM[gi], n_m(gi)), (C[gi], sC[gi], n_c(gi))
    E[go], L[go] = (C[go], sC[go], n_c(go)), (M[go], sM[go], n_m(go))
    order = [gi, go]

    te, ve = g.tensor, g.vector
    U = [T.U0, T.U1]
    PY = [T.PY0, T.PY1]
    te.wait_ge(S.sID, n_id)
    for i, grp in enumerate(order):
        piece, sem, cnt = E[grp]
        te.wait_ge(sem, cnt)
        for ch in (0, 1):
            te.matmul(T["NE%d%d" % (grp, ch)][:, 0:HC], T.ID[:, :], piece[:, ch * HC:(ch + 1) * HC],
                      True, True).then_inc(S["ne%d%d" % (grp, ch)], 1)
        ws, wc = w_wait(grp)
        te.wait_ge(ws, wc)
        for ch in (0, 1):
            te.matmul(PY[ch][:, 0:HC], W[grp][:, :], piece[:, ch * HC:(ch + 1) * HC], i == 0, False)
    for i, grp in enumerate(order):
        for ch in (0, 1):
            te.wait_ge(S["u%d%d" % (grp, ch)], 1)
            mm = te.matmul(PY[ch][:, 0:HC], W[grp][:, :], U[grp][:, ch * HC:(ch + 1) * HC], False, i == 1)
            if i == 1:
                mm.then_inc(S["sy%d" % ch], 1)
    for grp in order:
        piece, sem, cnt = L[grp]
        ve.wait_ge(sem, cnt)
        for ch in (0, 1):
            ve.wait_ge(S["ne%d%d" % (grp, ch)], 1)
            ve.tensor_tensor(U[grp][:, ch * HC:(ch + 1) * HC], T["NE%d%d" % (grp, ch)][:, 0:HC],
                             piece[:, ch * HC:(ch + 1) * HC], AluOpType.max).then_inc(S["u%d%d" % (grp, ch)], 1)
    for ch in (0, 1):
        ve.wait_ge(S["sy%d" % ch], 1)
        ve.tensor_copy(T.YS[:, ch * HC:(ch + 1) * HC], PY[ch][:, 0:HC]).then_inc(S["cp%d" % ch], 1)
    for ch, q in ((0, g.sync), (1, g.scalar)):
        q.wait_ge(S["cp%d" % ch], 1)
        q.dma_start(T.y[:, ch * HC:(ch + 1) * HC], T.YS[:, ch * HC:(ch + 1) * HC]).then_inc(S["st%d" % ch], 16)
        q.wait_ge(S["st%d" % ch], 16)
    g.wait_ge(S.sent, sent)
